import numpy as np
import ml_dtypes


def mxq(x, axis, fmt="e4m3"):
    dtype, down = {"e4m3": (ml_dtypes.float8_e4m3fn, 7), "e5m2": (ml_dtypes.float8_e5m2, 14)}[fmt]
    v = np.moveaxis(np.asarray(x, np.float32).astype(ml_dtypes.bfloat16).astype(np.float64), axis, -1)
    blocks = v.reshape(v.shape[:-1] + (-1, 32))
    amax = np.abs(blocks).max(-1, keepdims=True)
    byte = np.maximum(np.where(amax > 0, np.frexp(amax)[1] - 1 + 127, 0) - down, 1)
    scale = np.exp2(byte - 127.0)
    codes = (blocks / scale).astype(np.float32).astype(dtype).astype(np.float64)
    return np.moveaxis((codes * scale).reshape(v.shape), -1, axis)


WIDE = False


def mx_kscale(k):
    if not WIDE:
        return np.ones(k)
    levels = np.array([10, -10, 5, -5, 0])
    if k % 512:
        return np.exp2(np.random.permutation(np.resize(levels, k // 32))).repeat(32)
    a = np.empty((k // 512, 16))
    for p in range(k // 512):
        a[p, :8] = np.random.permutation(np.resize(levels, 8))
        for g in range(8):
            far = levels[np.abs(levels - a[p, g]) >= 10]
            a[p, g + 8] = far[np.random.randint(len(far))]
    return np.exp2(a.ravel()).repeat(32)


def f64(x):
    return np.asarray(x).astype(np.float64)


def striped(idx):
    return np.tile(np.asarray(idx).reshape(-1, 16).T, (8, 1)).astype(np.uint16)


def unstriped(offs):
    return offs[:16].T.reshape(-1).astype(np.int64)


E2M1 = np.array([0.0, 0.5, 1.0, 1.5, 2.0, 3.0, 4.0, 6.0, -0.0, -0.5, -1.0, -1.5, -2.0, -3.0, -4.0, -6.0])


def pack_weight(w, fmt):
    k, n = w.shape
    w = f64(np.asarray(w, np.float32).astype(ml_dtypes.bfloat16)).reshape(k // 32, 32, n)
    amax = np.abs(w).max(1)
    if fmt == "e4m3":
        byte = np.frexp(amax)[1] - 1 + 127 - 7
    else:
        mant, ex = np.frexp(amax / 6.0)
        byte = np.where(mant > 0.5, ex, ex - 1) + 127
    byte = np.clip(np.where(amax > 0, byte, 1), 1, 254)
    scaled = (w * np.exp2(127.0 - byte)[:, None, :]).reshape(k, n).astype(np.float32)
    by_word = np.ascontiguousarray(scaled.reshape(k // 512, 128, 4, n).transpose(0, 1, 3, 2))
    if fmt == "e4m3":
        words = by_word.astype(ml_dtypes.float8_e4m3fn).view(np.uint8)
    else:
        c = by_word.astype(ml_dtypes.float4_e2m1fn).view(np.uint8) & 0xF
        words = (c[..., 0::2] | (c[..., 1::2] << 4)).reshape(k // 512, 128, 2 * n)
    return np.ascontiguousarray(words), np.ascontiguousarray(byte.astype(np.uint8).reshape(k // 512, 16, n))


def unpack_weight(words, scales, fmt):
    g, _, n = scales.shape
    words = np.ascontiguousarray(words).reshape(g, 128, n, -1)
    if fmt == "e4m3":
        vals = words.view(ml_dtypes.float8_e4m3fn).astype(np.float64)
    else:
        nib = np.empty((g, 128, n, 4), np.uint8)
        nib[..., 0::2] = words & 0xF
        nib[..., 1::2] = words >> 4
        vals = E2M1[nib]
    vals = vals * np.repeat(np.exp2(scales.astype(np.float64) - 127.0), 8, axis=1)[..., None]
    return vals.transpose(0, 1, 3, 2).reshape(g * 512, n)


D, T, I, Q, U, G, M = 512, 2048, 512, 128, 1024, 64, 512


def setup_inputs():
    n = np.random.standard_normal
    idx = np.random.permutation(T)[:I]
    idx2 = np.random.permutation(U)[:I]
    idx3 = np.random.permutation(M)[:G]
    fd = mx_kscale(D)
    keysp = pack_weight(n((D, T)) / fd[:, None], "e2m1")
    return {
        "query": (n((D, Q)) * 0.7 / np.sqrt(D) * fd[:, None]).astype(np.float32),
        "query2": (n((D, Q)) * 0.7 / np.sqrt(D) * fd[:, None]).astype(np.float32),
        "keys_words": keysp[0],
        "keys_scales": keysp[1],
        "notes": (n((D, U)) / fd[:, None]).astype(np.float32),
        "worth": np.tile(np.random.uniform(0.2, 2.0, T), (128, 1)).astype(np.float32),
        "old": (1.0 * n((Q, M))).astype(np.float32),
        "offs": striped(idx),
        "offs2": striped(idx2),
        "offs3": striped(idx3),
    }


def reference(query, query2, keys_words, keys_scales, notes, worth, old, offs, offs2, offs3):
    idx = unstriped(offs)
    idx2 = unstriped(offs2)
    idx3 = unstriped(offs3)
    keysu = unpack_weight(keys_words, keys_scales, "e2m1")
    queryq = mxq(f64(query), 0, "e4m3")
    keysidxg = keysu[:, idx]
    query2q = mxq(f64(query2), 0, "e4m3")
    notesidx2q = mxq(f64(notes)[:, idx2], 0, "e4m3")
    s = queryq.T @ keysidxg + query2q.T @ notesidx2q
    w = np.maximum(s, 0.0)
    ws = w * f64(worth)[:1][:, idx] * 2.0
    wp = ws.reshape(Q, G, I // G).sum(axis=2)
    wf = np.zeros((Q, M))
    wf[:, idx3] = wp
    y = f64(old) + wf
    return y

@@ -1,0 +1,171 @@
+from contextlib import ExitStack
+
+import concourse.mybir as mybir
+from concourse.masks import make_identity
+
+F32 = mybir.dt.float32
+BF16 = mybir.dt.bfloat16
+I32 = mybir.dt.int32
+U32 = mybir.dt.uint32
+U16 = mybir.dt.uint16
+U8 = mybir.dt.uint8
+FP8X4 = mybir.dt.float8_e4m3fn_x4
+FP4X4 = mybir.dt.float4_e2m1fn_x4
+ALU = mybir.AluOpType
+COPY = mybir.ActivationFunctionType.Copy
+
+P = 128
+PACK = 4
+D, T, SLOTS, Q, U, RUNS, M = 512, 2048, 512, 128, 1024, 64, 512
+RUN = SLOTS // RUNS
+HALF = SLOTS // 2
+WORTH_ROW = P - 1
+VECTOR_SHARE = (256, 256, 0, 256)
+
+FLOPS = 2 * 2 * D * Q * SLOTS
+BYTES = 4 * (2 * D * Q + D * U + T + 2 * Q * M) + 2 * P * T + 16 * T + 2 * P * (32 + 32 + 4)
+
+
+def tile_attend_twosources_pagesums_lean_kernel(
+    tc, query, query2, keys_words, keys_scales, notes, worth, old, offs, offs2, offs3, out
+):
+    nc = tc.nc
+    with ExitStack() as ctx:
+        lists = ctx.enter_context(tc.tile_pool(name="lists", bufs=1))
+        sb = ctx.enter_context(tc.tile_pool(name="sb", bufs=1))
+        ps = ctx.enter_context(tc.psum_pool(name="ps", bufs=1))
+
+        tok_list = lists.tile([P, SLOTS // 16], U16, name="tok_list")
+        note_list = lists.tile([P, SLOTS // 16], U16, name="note_list")
+        col_list = lists.tile([P, RUNS // 16], U16, name="col_list")
+
+        key_scale_pool = sb.tile([P, T], U8, name="key_scale_pool", align_bytes=64)
+        worth_pool = sb.tile([P, T], F32, name="worth_pool", align_bytes=64)
+        key_word_pool = sb.tile([P, T], U16, name="key_word_pool", align_bytes=64)
+        note_planes = [sb.tile([P, U], F32, name="note_plane%d" % t, align_bytes=64) for t in range(PACK)]
+        q_raw = [sb.tile([P, PACK, Q], F32, name="q_raw%d" % j, align_bytes=64) for j in range(2)]
+        old_sb = sb.tile([P, M], F32, name="old_sb", align_bytes=64)
+        placed = sb.tile([P, M], F32, name="placed", align_bytes=64)
+        ident = sb.tile([P, P], F32, name="ident", align_bytes=64)
+
+        nc.gpsimd.memset(key_scale_pool[:].bitcast(I32), 0)
+        nc.vector.memset(worth_pool[0:WORTH_ROW, :], 0.0)
+        make_identity(nc, ident[:])
+        nc.gpsimd.memset(placed[:], 0.0)
+
+        notes_by_plane = notes.rearrange("(p t) u -> p t u", t=PACK)
+        nc.sync.dma_start(tok_list[:], offs)
+        nc.sync.dma_start(worth_pool[WORTH_ROW:P, :], worth[0:1, :])
+        nc.sync.dma_start(note_list[:], offs2)
+        for t in range(PACK):
+            nc.sync.dma_start(note_planes[t][:], notes_by_plane[:, t, :])
+            if t == 2:
+                for quad in range(4):
+                    nc.sync.dma_start(
+                        key_scale_pool[32 * quad : 32 * quad + 4, :].bitcast(I32),
+                        keys_scales[0, 4 * quad : 4 * quad + 4, :].bitcast(I32),
+                    )
+        nc.sync.dma_start(q_raw[1][:], query2.rearrange("(p t) q -> p t q", t=PACK))
+        nc.sync.dma_start(q_raw[0][:], query.rearrange("(p t) q -> p t q", t=PACK))
+        nc.sync.dma_start(key_word_pool[:].bitcast(I32), keys_words[0].bitcast(I32))
+        nc.sync.dma_start(col_list[:], offs3)
+        nc.sync.dma_start(old_sb[:], old)
+
+        def part(lst, lo, hi):
+            return lst[:, lo // 16 : hi // 16]
+
+        worth_row = sb.tile([P, SLOTS], F32, name="worth_row", align_bytes=64)
+        nc.vector.tensor_copy(worth_row[:], worth_pool[:].indirect(tok_list[:]))
+        turned = ps.tile([P, SLOTS // P, P], F32, name="turned")
+        for c in range(SLOTS // P):
+            nc.tensor.transpose(turned[:, c, :], worth_row[:, c * P : (c + 1) * P], ident[:])
+
+        key_scales = sb.tile([P, SLOTS], U8, name="key_scales", align_bytes=64)
+        picked = [sb.tile([P, PACK, HALF], BF16, name="picked%d" % h, align_bytes=64) for h in range(2)]
+
+        def gather_notes(engine, t, lo, hi):
+            for h in range(2):
+                a, b = max(lo, h * HALF), min(hi, (h + 1) * HALF)
+                if a < b:
+                    src = note_planes[t][:].indirect(part(note_list, a, b))
+                    dst = picked[h][:, t, a - h * HALF : b - h * HALF]
+                    if engine is nc.vector:
+                        nc.vector.tensor_copy(dst, src)
+                    else:
+                        nc.scalar.activation(dst, src, COPY)
+
+        worth2 = sb.tile([P, SLOTS], F32, name="worth2", align_bytes=64)
+        for t in range(PACK):
+            gather_notes(nc.vector, t, 0, VECTOR_SHARE[t])
+            gather_notes(nc.scalar, t, VECTOR_SHARE[t], SLOTS)
+            if t == 0:
+                worth_col = sb.tile([P, SLOTS // P], F32, name="worth_col", align_bytes=64)
+                nc.vector.tensor_scalar(worth_col[:], turned[:, :, WORTH_ROW], 2.0, None, ALU.mult)
+                spread = ps.tile([P, SLOTS], F32, name="spread")
+                for c in range(SLOTS // P):
+                    nc.tensor.transpose(
+                        spread[:, c * P : (c + 1) * P], worth_col[:, c : c + 1].to_broadcast([P, P]), ident[:]
+                    )
+            if t == 1:
+                nc.vector.tensor_copy(worth2[:], spread[:])
+                nc.vector.tensor_copy(key_scales[:], key_scale_pool[:].indirect(tok_list[:]))
+
+        woven = [sb.tile([P, HALF, PACK], BF16, name="woven%d" % h, align_bytes=64) for h in range(2)]
+        note_codes = [sb.tile([P, HALF], U32, name="note_codes%d" % h, align_bytes=64) for h in range(2)]
+        note_scales = [sb.tile([P, HALF], U8, name="note_scales%d" % h, align_bytes=64) for h in range(2)]
+        q_woven = [sb.tile([P, Q, PACK], BF16, name="q_woven%d" % j, align_bytes=64) for j in range(2)]
+        q_codes = [sb.tile([P, Q], U32, name="q_codes%d" % j, align_bytes=64) for j in range(2)]
+        q_scales = [sb.tile([P, Q], U8, name="q_scales%d" % j, align_bytes=64) for j in range(2)]
+        key_words = [sb.tile([P, HALF], U16, name="key_words%d" % h, align_bytes=64) for h in range(2)]
+        scores = [ps.tile([P, HALF], F32, name="scores%d" % h) for h in range(2)]
+
+        def quantise(codes, scales, src):
+            nc.vector.quantize_mx(out=codes[:].bitcast(FP8X4), scales=scales[:], in_=src[:].rearrange("p c t -> p (c t)"))
+
+        def product(h, j, start):
+            rhs = key_words[h][:].bitcast(FP4X4) if j == 0 else note_codes[h][:].bitcast(FP8X4)
+            rhs_scale = key_scales[:, h * HALF : (h + 1) * HALF] if j == 0 else note_scales[h][:]
+            nc.tensor.matmul_mx(
+                out=scores[h][:],
+                lhsT=q_codes[j][:].bitcast(FP8X4),
+                lhsT_scale=q_scales[j][:],
+                rhs=rhs,
+                rhs_scale=rhs_scale,
+                start=start,
+                stop=not start,
+            )
+
+        nc.vector.tensor_copy(woven[0][:], picked[0][:].rearrange("p t s -> p s t"))
+        nc.scalar.copy(woven[1][:], picked[1][:].rearrange("p t s -> p s t"))
+        nc.vector.tensor_copy(q_woven[0][:], q_raw[0][:].rearrange("p t q -> p q t"))
+        nc.scalar.copy(q_woven[1][:], q_raw[1][:].rearrange("p t q -> p q t"))
+        quantise(note_codes[0], note_scales[0], woven[0])
+        quantise(q_codes[0], q_scales[0], q_woven[0])
+        quantise(note_codes[1], note_scales[1], woven[1])
+        nc.vector.tensor_copy(key_words[0][:], key_word_pool[:].indirect(part(tok_list, 0, HALF)))
+        product(0, 0, True)
+        quantise(q_codes[1], q_scales[1], q_woven[1])
+        product(0, 1, False)
+        product(1, 1, True)
+        nc.vector.tensor_copy(key_words[1][:], key_word_pool[:].indirect(part(tok_list, HALF, SLOTS)))
+        product(1, 0, False)
+
+        weighted = [sb.tile([P, HALF], F32, name="weighted%d" % h, align_bytes=64) for h in range(2)]
+        run_sums = sb.tile([P, RUNS], F32, name="run_sums", align_bytes=64)
+        for h in range(2):
+            nc.vector.scalar_tensor_tensor(
+                weighted[h][:], scores[h][:], 0.0, worth2[:, h * HALF : (h + 1) * HALF], ALU.max, ALU.mult
+            )
+        for h in range(2):
+            nc.vector.tensor_reduce(
+                run_sums[:, h * (RUNS // 2) : (h + 1) * (RUNS // 2)],
+                weighted[h][:].rearrange("p (g r) -> p g r", r=RUN),
+                mybir.AxisListType.X,
+                ALU.add,
+            )
+        nc.vector.tensor_copy(placed[:].indirect(col_list[:]), run_sums[:])
+        result = [sb.tile([P, M // 2], F32, name="result%d" % h, align_bytes=64) for h in range(2)]
+        for h in range(2):
+            cols = slice(h * (M // 2), (h + 1) * (M // 2))
+            nc.vector.tensor_tensor(result[h][:], placed[:, cols], old_sb[:, cols], ALU.add)
+            (nc.sync if h == 0 else nc.scalar).dma_start(out[:, cols], result[h][:])

@@ -52,6 +52,9 @@ def tile_attend_twosources_pagesums_lean_kernel(
         nc.vector.memset(worth_pool[0:WORTH_ROW, :], 0.0)
         make_identity(nc, ident[:])
         nc.gpsimd.memset(placed[:], 0.0)
+        warm = sb.tile([P, 8], F32, name="warm")
+        nc.vector.memset(warm[:, 0:1], 0.0)
+        nc.scalar.activation(warm[:, 4:5], warm[:, 0:1], COPY)
 
         notes_by_plane = notes.rearrange("(p t) u -> p t u", t=PACK)
         nc.sync.dma_start(tok_list[:], offs)

@@ -20,7 +20,8 @@ D, T, SLOTS, Q, U, RUNS, M = 512, 2048, 512, 128, 1024, 64, 512
 RUN = SLOTS // RUNS
 HALF = SLOTS // 2
 WORTH_ROW = P - 1
-VECTOR_SHARE = (256, 256, 0, 256)
+SCALE_ROW = 48
+VECTOR_SLOTS = 320
 
 FLOPS = 2 * 2 * D * Q * SLOTS
 BYTES = 4 * (2 * D * Q + D * U + T + 2 * Q * M) + 2 * P * T + 16 * T + 2 * P * (32 + 32 + 4)
@@ -39,83 +40,79 @@ def tile_attend_twosources_pagesums_lean_kernel(
         note_list = lists.tile([P, SLOTS // 16], U16, name="note_list")
         col_list = lists.tile([P, RUNS // 16], U16, name="col_list")
 
-        key_scale_pool = sb.tile([P, T], U8, name="key_scale_pool", align_bytes=64)
+        key_scale_pool = sb.tile([P, T], U8, name="key_scale_pool", tag="scales_then_old", align_bytes=64)
         worth_pool = sb.tile([P, T], F32, name="worth_pool", align_bytes=64)
         key_word_pool = sb.tile([P, T], U16, name="key_word_pool", align_bytes=64)
         note_planes = [sb.tile([P, U], F32, name="note_plane%d" % t, align_bytes=64) for t in range(PACK)]
-        q_raw = [sb.tile([P, PACK, Q], F32, name="q_raw%d" % j, align_bytes=64) for j in range(2)]
-        old_sb = sb.tile([P, M], F32, name="old_sb", align_bytes=64)
+        q_raw = [
+            sb.tile([P, PACK, Q], F32, name="q_raw0", tag="query_then_worth", align_bytes=64),
+            sb.tile([P, PACK, Q], F32, name="q_raw1", align_bytes=64),
+        ]
+        key_scales = sb.tile([P, SLOTS], U8, name="key_scales", align_bytes=64)
         placed = sb.tile([P, M], F32, name="placed", align_bytes=64)
         ident = sb.tile([P, P], F32, name="ident", align_bytes=64)
 
-        nc.gpsimd.memset(key_scale_pool[:].bitcast(I32), 0)
-        nc.vector.memset(worth_pool[0:WORTH_ROW, :], 0.0)
-        make_identity(nc, ident[:])
-        nc.gpsimd.memset(placed[:], 0.0)
+        notes_by_plane = notes.rearrange("(p t) u -> p t u", t=PACK)
+
+        nc.gpsimd.memset(key_scale_pool[0:SCALE_ROW, :].bitcast(I32), 0)
+        nc.gpsimd.memset(key_scale_pool[SCALE_ROW + 16 : P, :].bitcast(I32), 0)
         warm = sb.tile([P, 8], F32, name="warm")
         nc.vector.memset(warm[:, 0:1], 0.0)
         nc.scalar.activation(warm[:, 4:5], warm[:, 0:1], COPY)
+        nc.vector.memset(worth_pool[0:WORTH_ROW, :], 0.0)
+        make_identity(nc, ident[:])
+        nc.gpsimd.memset(key_scales[:].bitcast(I32), 0)
+        nc.gpsimd.memset(placed[:], 0.0)
 
-        notes_by_plane = notes.rearrange("(p t) u -> p t u", t=PACK)
         nc.sync.dma_start(tok_list[:], offs)
+        nc.sync.dma_start(key_scale_pool[SCALE_ROW : SCALE_ROW + 16, :].bitcast(I32), keys_scales[0].bitcast(I32))
         nc.sync.dma_start(worth_pool[WORTH_ROW:P, :], worth[0:1, :])
         nc.sync.dma_start(note_list[:], offs2)
         for t in range(PACK):
             nc.sync.dma_start(note_planes[t][:], notes_by_plane[:, t, :])
-            if t == 2:
-                for quad in range(4):
-                    nc.sync.dma_start(
-                        key_scale_pool[32 * quad : 32 * quad + 4, :].bitcast(I32),
-                        keys_scales[0, 4 * quad : 4 * quad + 4, :].bitcast(I32),
-                    )
         nc.sync.dma_start(q_raw[1][:], query2.rearrange("(p t) q -> p t q", t=PACK))
         nc.sync.dma_start(q_raw[0][:], query.rearrange("(p t) q -> p t q", t=PACK))
         nc.sync.dma_start(key_word_pool[:].bitcast(I32), keys_words[0].bitcast(I32))
         nc.sync.dma_start(col_list[:], offs3)
-        nc.sync.dma_start(old_sb[:], old)
 
-        def part(lst, lo, hi):
-            return lst[:, lo // 16 : hi // 16]
+        def half_list(lst, h):
+            return lst[:, h * (HALF // 16) : (h + 1) * (HALF // 16)]
 
         worth_row = sb.tile([P, SLOTS], F32, name="worth_row", align_bytes=64)
-        nc.vector.tensor_copy(worth_row[:], worth_pool[:].indirect(tok_list[:]))
+        picked_scales = sb.tile([P, SLOTS], U8, name="picked_scales", align_bytes=64)
+        nc.vector.tensor_copy(picked_scales[:], key_scale_pool[:].indirect(tok_list[:]))
+        for quad in range(4):
+            nc.sync.dma_start(
+                key_scales[32 * quad : 32 * quad + 4, :].bitcast(I32),
+                picked_scales[SCALE_ROW + 4 * quad : SCALE_ROW + 4 * quad + 4, :].bitcast(I32),
+            )
+        old_sb = sb.tile([P, M], F32, name="old_sb", tag="scales_then_old", align_bytes=64)
+        nc.sync.dma_start(old_sb[:], old)
+        nc.scalar.activation(worth_row[:], worth_pool[:].indirect(tok_list[:]), COPY)
         turned = ps.tile([P, SLOTS // P, P], F32, name="turned")
         for c in range(SLOTS // P):
             nc.tensor.transpose(turned[:, c, :], worth_row[:, c * P : (c + 1) * P], ident[:])
 
-        key_scales = sb.tile([P, SLOTS], U8, name="key_scales", align_bytes=64)
-        picked = [sb.tile([P, PACK, HALF], BF16, name="picked%d" % h, align_bytes=64) for h in range(2)]
-
-        def gather_notes(engine, t, lo, hi):
-            for h in range(2):
-                a, b = max(lo, h * HALF), min(hi, (h + 1) * HALF)
-                if a < b:
-                    src = note_planes[t][:].indirect(part(note_list, a, b))
-                    dst = picked[h][:, t, a - h * HALF : b - h * HALF]
-                    if engine is nc.vector:
-                        nc.vector.tensor_copy(dst, src)
-                    else:
-                        nc.scalar.activation(dst, src, COPY)
-
-        worth2 = sb.tile([P, SLOTS], F32, name="worth2", align_bytes=64)
+        picked = sb.tile([P, PACK, SLOTS - VECTOR_SLOTS], BF16, name="picked", align_bytes=64)
+        woven = sb.tile([P, SLOTS, PACK], BF16, name="woven", align_bytes=64)
+        worth_col = sb.tile([P, SLOTS // P], F32, name="worth_col", align_bytes=64)
+        spread = ps.tile([P, SLOTS], F32, name="spread")
         for t in range(PACK):
-            gather_notes(nc.vector, t, 0, VECTOR_SHARE[t])
-            gather_notes(nc.scalar, t, VECTOR_SHARE[t], SLOTS)
+            nc.vector.tensor_copy(
+                woven[:, 0:VECTOR_SLOTS, t], note_planes[t][:].indirect(note_list[:, 0 : VECTOR_SLOTS // 16])
+            )
+            nc.scalar.activation(
+                picked[:, t, :], note_planes[t][:].indirect(note_list[:, VECTOR_SLOTS // 16 : SLOTS // 16]), COPY
+            )
             if t == 0:
-                worth_col = sb.tile([P, SLOTS // P], F32, name="worth_col", align_bytes=64)
-                nc.vector.tensor_scalar(worth_col[:], turned[:, :, WORTH_ROW], 2.0, None, ALU.mult)
-                spread = ps.tile([P, SLOTS], F32, name="spread")
+                nc.scalar.activation(worth_col[:], turned[:, :, WORTH_ROW], COPY, scale=2.0)
                 for c in range(SLOTS // P):
                     nc.tensor.transpose(
                         spread[:, c * P : (c + 1) * P], worth_col[:, c : c + 1].to_broadcast([P, P]), ident[:]
                     )
-            if t == 1:
-                nc.vector.tensor_copy(worth2[:], spread[:])
-                nc.vector.tensor_copy(key_scales[:], key_scale_pool[:].indirect(tok_list[:]))
 
-        woven = [sb.tile([P, HALF, PACK], BF16, name="woven%d" % h, align_bytes=64) for h in range(2)]
-        note_codes = [sb.tile([P, HALF], U32, name="note_codes%d" % h, align_bytes=64) for h in range(2)]
-        note_scales = [sb.tile([P, HALF], U8, name="note_scales%d" % h, align_bytes=64) for h in range(2)]
+        note_codes = sb.tile([P, SLOTS], U32, name="note_codes", align_bytes=64)
+        note_scales = sb.tile([P, SLOTS], U8, name="note_scales", align_bytes=64)
         q_woven = [sb.tile([P, Q, PACK], BF16, name="q_woven%d" % j, align_bytes=64) for j in range(2)]
         q_codes = [sb.tile([P, Q], U32, name="q_codes%d" % j, align_bytes=64) for j in range(2)]
         q_scales = [sb.tile([P, Q], U8, name="q_scales%d" % j, align_bytes=64) for j in range(2)]
@@ -126,8 +123,8 @@ def tile_attend_twosources_pagesums_lean_kernel(
             nc.vector.quantize_mx(out=codes[:].bitcast(FP8X4), scales=scales[:], in_=src[:].rearrange("p c t -> p (c t)"))
 
         def product(h, j, start):
-            rhs = key_words[h][:].bitcast(FP4X4) if j == 0 else note_codes[h][:].bitcast(FP8X4)
-            rhs_scale = key_scales[:, h * HALF : (h + 1) * HALF] if j == 0 else note_scales[h][:]
+            rhs = key_words[h][:].bitcast(FP4X4) if j == 0 else note_codes[:, h * HALF : (h + 1) * HALF].bitcast(FP8X4)
+            rhs_scale = key_scales[:, h * HALF : (h + 1) * HALF] if j == 0 else note_scales[:, h * HALF : (h + 1) * HALF]
             nc.tensor.matmul_mx(
                 out=scores[h][:],
                 lhsT=q_codes[j][:].bitcast(FP8X4),
@@ -138,19 +135,22 @@ def tile_attend_twosources_pagesums_lean_kernel(
                 stop=not start,
             )
 
-        nc.vector.tensor_copy(woven[0][:], picked[0][:].rearrange("p t s -> p s t"))
-        nc.scalar.copy(woven[1][:], picked[1][:].rearrange("p t s -> p s t"))
-        nc.vector.tensor_copy(q_woven[0][:], q_raw[0][:].rearrange("p t q -> p q t"))
-        nc.scalar.copy(q_woven[1][:], q_raw[1][:].rearrange("p t q -> p q t"))
-        quantise(note_codes[0], note_scales[0], woven[0])
-        quantise(q_codes[0], q_scales[0], q_woven[0])
-        quantise(note_codes[1], note_scales[1], woven[1])
-        nc.vector.tensor_copy(key_words[0][:], key_word_pool[:].indirect(part(tok_list, 0, HALF)))
-        product(0, 0, True)
+        def weave(copy, dst, src):
+            copy(dst.rearrange("p (c i) t -> p c t i", i=4), src.rearrange("p t (c i) -> p c t i", i=4))
+
+        weave(nc.scalar.copy, woven[:, VECTOR_SLOTS:SLOTS, :], picked[:])
+        weave(nc.vector.tensor_copy, q_woven[1][:], q_raw[1][:])
+        weave(nc.scalar.copy, q_woven[0][:], q_raw[0][:])
+        worth2 = sb.tile([P, SLOTS], F32, name="worth2", tag="query_then_worth", align_bytes=64)
+        nc.scalar.copy(worth2[:], spread[:])
         quantise(q_codes[1], q_scales[1], q_woven[1])
-        product(0, 1, False)
-        product(1, 1, True)
-        nc.vector.tensor_copy(key_words[1][:], key_word_pool[:].indirect(part(tok_list, HALF, SLOTS)))
+        quantise(note_codes, note_scales, woven)
+        for h in range(2):
+            product(h, 1, True)
+        nc.vector.tensor_copy(key_words[0][:], key_word_pool[:].indirect(half_list(tok_list, 0)))
+        quantise(q_codes[0], q_scales[0], q_woven[0])
+        product(0, 0, False)
+        nc.vector.tensor_copy(key_words[1][:], key_word_pool[:].indirect(half_list(tok_list, 1)))
         product(1, 0, False)
 
         weighted = [sb.tile([P, HALF], F32, name="weighted%d" % h, align_bytes=64) for h in range(2)]

from contextlib import ExitStack

import concourse.mybir as mybir
from concourse.masks import make_identity

F32 = mybir.dt.float32
BF16 = mybir.dt.bfloat16
I32 = mybir.dt.int32
U32 = mybir.dt.uint32
U16 = mybir.dt.uint16
U8 = mybir.dt.uint8
FP8X4 = mybir.dt.float8_e4m3fn_x4
FP4X4 = mybir.dt.float4_e2m1fn_x4
ALU = mybir.AluOpType
COPY = mybir.ActivationFunctionType.Copy

P = 128
PACK = 4
D, T, SLOTS, Q, U, RUNS, M = 512, 2048, 512, 128, 1024, 64, 512
RUN = SLOTS // RUNS
HALF = SLOTS // 2
WORTH_ROW = P - 1
SCALE_ROW = 48
VECTOR_SLOTS = 320

FLOPS = 2 * 2 * D * Q * SLOTS
BYTES = 4 * (2 * D * Q + D * U + T + 2 * Q * M) + 2 * P * T + 16 * T + 2 * P * (32 + 32 + 4)


def tile_attend_twosources_pagesums_lean_kernel(
    tc, query, query2, keys_words, keys_scales, notes, worth, old, offs, offs2, offs3, out
):
    nc = tc.nc
    with ExitStack() as ctx:
        lists = ctx.enter_context(tc.tile_pool(name="lists", bufs=1))
        sb = ctx.enter_context(tc.tile_pool(name="sb", bufs=1))
        ps = ctx.enter_context(tc.psum_pool(name="ps", bufs=1))

        tok_list = lists.tile([P, SLOTS // 16], U16, name="tok_list")
        note_list = lists.tile([P, SLOTS // 16], U16, name="note_list")
        col_list = lists.tile([P, RUNS // 16], U16, name="col_list")

        key_scale_pool = sb.tile([P, T], U8, name="key_scale_pool", tag="scales_then_old", align_bytes=64)
        worth_pool = sb.tile([P, T], F32, name="worth_pool", align_bytes=64)
        key_word_pool = sb.tile([P, T], U16, name="key_word_pool", align_bytes=64)
        note_planes = [sb.tile([P, U], F32, name="note_plane%d" % t, align_bytes=64) for t in range(PACK)]
        q_raw = [
            sb.tile([P, PACK, Q], F32, name="q_raw0", tag="query_then_worth", align_bytes=64),
            sb.tile([P, PACK, Q], F32, name="q_raw1", align_bytes=64),
        ]
        key_scales = sb.tile([P, SLOTS], U8, name="key_scales", align_bytes=64)
        placed = sb.tile([P, M], F32, name="placed", align_bytes=64)
        ident = sb.tile([P, P], F32, name="ident", align_bytes=64)

        notes_by_plane = notes.rearrange("(p t) u -> p t u", t=PACK)

        nc.gpsimd.memset(key_scale_pool[0:SCALE_ROW, :].bitcast(I32), 0)
        nc.gpsimd.memset(key_scale_pool[SCALE_ROW + 16 : P, :].bitcast(I32), 0)
        warm = sb.tile([P, 8], F32, name="warm")
        nc.vector.memset(warm[:, 0:1], 0.0)
        nc.scalar.activation(warm[:, 4:5], warm[:, 0:1], COPY)
        nc.vector.memset(worth_pool[0:WORTH_ROW, :], 0.0)
        make_identity(nc, ident[:])
        nc.gpsimd.memset(key_scales[:].bitcast(I32), 0)
        nc.gpsimd.memset(placed[:], 0.0)

        nc.sync.dma_start(tok_list[:], offs)
        nc.sync.dma_start(key_scale_pool[SCALE_ROW : SCALE_ROW + 16, :].bitcast(I32), keys_scales[0].bitcast(I32))
        nc.sync.dma_start(worth_pool[WORTH_ROW:P, :], worth[0:1, :])
        nc.sync.dma_start(note_list[:], offs2)
        for t in range(PACK):
            nc.sync.dma_start(note_planes[t][:], notes_by_plane[:, t, :])
        nc.sync.dma_start(q_raw[1][:], query2.rearrange("(p t) q -> p t q", t=PACK))
        nc.sync.dma_start(q_raw[0][:], query.rearrange("(p t) q -> p t q", t=PACK))
        nc.sync.dma_start(key_word_pool[:].bitcast(I32), keys_words[0].bitcast(I32))
        nc.sync.dma_start(col_list[:], offs3)

        def half_list(lst, h):
            return lst[:, h * (HALF // 16) : (h + 1) * (HALF // 16)]

        worth_row = sb.tile([P, SLOTS], F32, name="worth_row", align_bytes=64)
        picked_scales = sb.tile([P, SLOTS], U8, name="picked_scales", align_bytes=64)
        nc.vector.tensor_copy(picked_scales[:], key_scale_pool[:].indirect(tok_list[:]))
        for quad in range(4):
            nc.sync.dma_start(
                key_scales[32 * quad : 32 * quad + 4, :].bitcast(I32),
                picked_scales[SCALE_ROW + 4 * quad : SCALE_ROW + 4 * quad + 4, :].bitcast(I32),
            )
        old_sb = sb.tile([P, M], F32, name="old_sb", tag="scales_then_old", align_bytes=64)
        nc.sync.dma_start(old_sb[:], old)
        nc.scalar.activation(worth_row[:], worth_pool[:].indirect(tok_list[:]), COPY)
        turned = ps.tile([P, SLOTS // P, P], F32, name="turned")
        for c in range(SLOTS // P):
            nc.tensor.transpose(turned[:, c, :], worth_row[:, c * P : (c + 1) * P], ident[:])

        picked = sb.tile([P, PACK, SLOTS - VECTOR_SLOTS], BF16, name="picked", align_bytes=64)
        woven = sb.tile([P, SLOTS, PACK], BF16, name="woven", align_bytes=64)
        worth_col = sb.tile([P, SLOTS // P], F32, name="worth_col", align_bytes=64)
        spread = ps.tile([P, SLOTS], F32, name="spread")
        for t in range(PACK):
            nc.vector.tensor_copy(
                woven[:, 0:VECTOR_SLOTS, t], note_planes[t][:].indirect(note_list[:, 0 : VECTOR_SLOTS // 16])
            )
            nc.scalar.activation(
                picked[:, t, :], note_planes[t][:].indirect(note_list[:, VECTOR_SLOTS // 16 : SLOTS // 16]), COPY
            )
            if t == 0:
                nc.scalar.activation(worth_col[:], turned[:, :, WORTH_ROW], COPY, scale=2.0)
                for c in range(SLOTS // P):
                    nc.tensor.transpose(
                        spread[:, c * P : (c + 1) * P], worth_col[:, c : c + 1].to_broadcast([P, P]), ident[:]
                    )

        note_codes = sb.tile([P, SLOTS], U32, name="note_codes", align_bytes=64)
        note_scales = sb.tile([P, SLOTS], U8, name="note_scales", align_bytes=64)
        q_woven = [sb.tile([P, Q, PACK], BF16, name="q_woven%d" % j, align_bytes=64) for j in range(2)]
        q_codes = [sb.tile([P, Q], U32, name="q_codes%d" % j, align_bytes=64) for j in range(2)]
        q_scales = [sb.tile([P, Q], U8, name="q_scales%d" % j, align_bytes=64) for j in range(2)]
        key_words = [sb.tile([P, HALF], U16, name="key_words%d" % h, align_bytes=64) for h in range(2)]
        scores = [ps.tile([P, HALF], F32, name="scores%d" % h) for h in range(2)]

        def quantise(codes, scales, src):
            nc.vector.quantize_mx(out=codes[:].bitcast(FP8X4), scales=scales[:], in_=src[:].rearrange("p c t -> p (c t)"))

        def product(h, j, start):
            rhs = key_words[h][:].bitcast(FP4X4) if j == 0 else note_codes[:, h * HALF : (h + 1) * HALF].bitcast(FP8X4)
            rhs_scale = key_scales[:, h * HALF : (h + 1) * HALF] if j == 0 else note_scales[:, h * HALF : (h + 1) * HALF]
            nc.tensor.matmul_mx(
                out=scores[h][:],
                lhsT=q_codes[j][:].bitcast(FP8X4),
                lhsT_scale=q_scales[j][:],
                rhs=rhs,
                rhs_scale=rhs_scale,
                start=start,
                stop=not start,
            )

        def weave(copy, dst, src):
            copy(dst.rearrange("p (c i) t -> p c t i", i=4), src.rearrange("p t (c i) -> p c t i", i=4))

        weave(nc.scalar.copy, woven[:, VECTOR_SLOTS:SLOTS, :], picked[:])
        weave(nc.vector.tensor_copy, q_woven[1][:], q_raw[1][:])
        weave(nc.scalar.copy, q_woven[0][:], q_raw[0][:])
        worth2 = sb.tile([P, SLOTS], F32, name="worth2", tag="query_then_worth", align_bytes=64)
        nc.scalar.copy(worth2[:], spread[:])
        quantise(q_codes[1], q_scales[1], q_woven[1])
        quantise(note_codes, note_scales, woven)
        for h in range(2):
            product(h, 1, True)
        nc.vector.tensor_copy(key_words[0][:], key_word_pool[:].indirect(half_list(tok_list, 0)))
        quantise(q_codes[0], q_scales[0], q_woven[0])
        product(0, 0, False)
        nc.vector.tensor_copy(key_words[1][:], key_word_pool[:].indirect(half_list(tok_list, 1)))
        product(1, 0, False)

        weighted = [sb.tile([P, HALF], F32, name="weighted%d" % h, align_bytes=64) for h in range(2)]
        run_sums = sb.tile([P, RUNS], F32, name="run_sums", align_bytes=64)
        for h in range(2):
            nc.vector.scalar_tensor_tensor(
                weighted[h][:], scores[h][:], 0.0, worth2[:, h * HALF : (h + 1) * HALF], ALU.max, ALU.mult
            )
        for h in range(2):
            nc.vector.tensor_reduce(
                run_sums[:, h * (RUNS // 2) : (h + 1) * (RUNS // 2)],
                weighted[h][:].rearrange("p (g r) -> p g r", r=RUN),
                mybir.AxisListType.X,
                ALU.add,
            )
        nc.vector.tensor_copy(placed[:].indirect(col_list[:]), run_sums[:])
        result = [sb.tile([P, M // 2], F32, name="result%d" % h, align_bytes=64) for h in range(2)]
        for h in range(2):
            cols = slice(h * (M // 2), (h + 1) * (M // 2))
            nc.vector.tensor_tensor(result[h][:], placed[:, cols], old_sb[:, cols], ALU.add)
            (nc.sync if h == 0 else nc.scalar).dma_start(out[:, cols], result[h][:])
